import numpy as np
import ml_dtypes


def mxq(x, axis, fmt="e4m3"):
    dtype, down = {"e4m3": (ml_dtypes.float8_e4m3fn, 7), "e5m2": (ml_dtypes.float8_e5m2, 14)}[fmt]
    v = np.moveaxis(np.asarray(x, np.float32).astype(ml_dtypes.bfloat16).astype(np.float64), axis, -1)
    blocks = v.reshape(v.shape[:-1] + (-1, 32))
    amax = np.abs(blocks).max(-1, keepdims=True)
    byte = np.maximum(np.where(amax > 0, np.frexp(amax)[1] - 1 + 127, 0) - down, 1)
    scale = np.exp2(byte - 127.0)
    codes = (blocks / scale).astype(np.float32).astype(dtype).astype(np.float64)
    return np.moveaxis((codes * scale).reshape(v.shape), -1, axis)


WIDE = False


def mx_kscale(k):
    if not WIDE:
        return np.ones(k)
    levels = np.array([10, -10, 5, -5, 0])
    if k % 512:
        return np.exp2(np.random.permutation(np.resize(levels, k // 32))).repeat(32)
    a = np.empty((k // 512, 16))
    for p in range(k // 512):
        a[p, :8] = np.random.permutation(np.resize(levels, 8))
        for g in range(8):
            far = levels[np.abs(levels - a[p, g]) >= 10]
            a[p, g + 8] = far[np.random.randint(len(far))]
    return np.exp2(a.ravel()).repeat(32)


def f64(x):
    return np.asarray(x).astype(np.float64)


def striped(idx):
    return np.tile(idx.reshape(-1, 16).T, (8, 1)).astype(np.uint16)


def unstriped(offs):
    return offs[:16].T.reshape(-1).astype(np.int64)


def striped8(idx):
    return np.concatenate([x.reshape(-1, 16).T for x in idx]).astype(np.uint16)


def runs(offs, k):
    lists = np.stack([offs[16 * r : 16 * r + 16].T.reshape(-1) for r in range(8)]).astype(np.int64)
    return lists[np.arange(k) % 512 // 64]


def pack_weight(w):
    k, n = w.shape
    w = f64(np.asarray(w, np.float32).astype(ml_dtypes.bfloat16)).reshape(k // 32, 32, n)
    amax = np.abs(w).max(1)
    byte = np.clip(np.where(amax > 0, np.frexp(amax)[1] - 1 + 127 - 7, 1), 1, 254)
    scaled = (w * np.exp2(127.0 - byte)[:, None, :]).reshape(k, n).astype(np.float32)
    words = np.ascontiguousarray(scaled.reshape(k // 512, 128, 4, n).transpose(0, 1, 3, 2)).astype(ml_dtypes.float8_e4m3fn).view(np.uint8)
    return words, np.ascontiguousarray(byte.astype(np.uint8).reshape(k // 512, 16, n))


def unpack_weight(words, scales):
    g, p, n, _ = words.shape
    vals = np.ascontiguousarray(words).view(ml_dtypes.float8_e4m3fn).astype(np.float64) * np.repeat(np.exp2(scales.astype(np.float64) - 127.0), 8, axis=1)[..., None]
    return vals.transpose(0, 1, 3, 2).reshape(g * 512, n)


def sigmoid(v):
    return 1.0 / (1.0 + np.exp(-np.maximum(v, -700.0)))

def planes(y):
    n, m = y.shape
    v = y.astype(np.float32).astype(ml_dtypes.bfloat16).astype(np.float64).reshape(n // 32, 32, m)
    top = np.abs(v).max(1)
    byte = np.clip(np.where(top > 0, np.frexp(top)[1] - 1 + 127 - 7, 1), 1, 254)
    codes = (v * np.exp2(127.0 - byte)[:, None, :]).reshape(n, m).astype(np.float32).astype(ml_dtypes.float8_e4m3fn).view(np.uint8)
    words = codes.reshape(n // 512, 128, 4, m).transpose(0, 1, 3, 2)
    return np.ascontiguousarray(words), np.ascontiguousarray(byte.astype(np.uint8).reshape(n // 512, 16, m))


K, T, S, N, H, W = 512, 2048, 512, 512, 512, 256


def setup_inputs():
    n = np.random.standard_normal
    s = mx_kscale(K)[:, None]
    u = mx_kscale(S)
    packed_xT = pack_weight(n((K, T)) * s)
    perm = np.stack([np.random.permutation(H) for _ in range(8)])
    return {
        "x_words": packed_xT[0],
        "x_scales": packed_xT[1],
        "wa": (n((K, H)) / np.sqrt(K) / s).astype(np.float32),
        "wb": (n((K, N)) / np.sqrt(K) / s).astype(np.float32),
        "gt": (np.random.uniform(0.5, 1.5, (S, 1)) * u[:, None]).astype(np.float32),
        "gi": (np.random.uniform(0.5, 1.5, (S, 1)) / u[:, None]).astype(np.float32),
        "offs": striped(np.random.permutation(T)[:S]),
        "two": striped(np.random.permutation(T)[:S]),
        "n1": striped8(perm[:, :W]),
        "n2": striped8(perm[:, W:]),
        "n3": striped8(np.stack([np.random.permutation(N) for _ in range(8)])),
        "n4": striped8(np.stack([np.random.permutation(N) for _ in range(8)])),
    }


def reference(x_words, x_scales, wa, wb, gt, gi, offs, two, n1, n2, n3, n4):
    xq = unpack_weight(x_words, x_scales)[:, unstriped(offs)]
    a = xq.T @ mxq(f64(wa), 0, "e4m3")
    pb = a[np.arange(S)[:, None], runs(n2, S)]
    pa = a[np.arange(S)[:, None], runs(n1, S)]
    rb = pb * sigmoid(pb - pa)
    ra = pa * sigmoid(pa - pb)
    ds = np.zeros((S, H))
    ds[np.arange(S)[:, None], runs(n1, S)] = ra
    dt = ds.copy()
    dt[np.arange(S)[:, None], runs(n2, S)] = rb
    z = f64(gt) * dt
    x_two = unpack_weight(x_words, x_scales)[:, unstriped(two)]
    b = x_two.T @ mxq(f64(wb), 0, "e4m3")
    z2 = f64(gi) * b
    cv = 0.0625 * ((mxq(z, 0, "e4m3").T @ mxq(z2, 0, "e4m3")))
    st = np.maximum(cv, cv[np.arange(H)[:, None], runs(n3, H)])
    out_0 = np.minimum(st, st[np.arange(H)[:, None], runs(n4, H)])
    return (out_0,) + planes(out_0)

@@ -1,0 +1,233 @@
+from contextlib import ExitStack
+
+import concourse.mybir as mybir
+from concourse.masks import make_identity
+
+K, T, S, N, H, W = 512, 2048, 512, 512, 512, 256
+FLOPS = 2 * K * S * H + 2 * K * S * N + 2 * S * H * N
+
+F32 = mybir.dt.float32
+BF16 = mybir.dt.bfloat16
+I32 = mybir.dt.int32
+U32 = mybir.dt.uint32
+U16 = mybir.dt.uint16
+U8 = mybir.dt.uint8
+FP8X4 = mybir.dt.float8_e4m3fn_x4
+ALU = mybir.AluOpType
+ACT = mybir.ActivationFunctionType
+
+P = 128
+PACK = 4
+
+
+def tile_picked_momduelhopmn_none_po_kernel(
+    tc, x_words, x_scales, wa, wb, gt, gi, offs, two, n1, n2, n3, n4, out_0, out_1, out_2
+):
+    nc = tc.nc
+    with ExitStack() as ctx:
+        keep = ctx.enter_context(tc.tile_pool(name="keep", bufs=1))
+        psum = ctx.enter_context(tc.psum_pool(name="psum", bufs=8))
+
+        def sb(shape, dtype, name, tag=""):
+            return keep.tile(shape, dtype, name=name, tag=tag, align_bytes=64)
+
+        def bank(name):
+            return psum.tile([P, 512], F32, name=name, tag="bank")
+
+        def load_list(src, name):
+            tile = keep.tile(list(src.shape), U16, name=name)
+            nc.sync.dma_start(tile[:], src)
+            return tile
+
+        x_bytes = sb([P, T], U8, "x_bytes")
+        nc.vector.memset(x_bytes[:].bitcast(I32), 0)
+        gate_rows = sb([P, P], F32, "gate_rows")
+        nc.vector.memset(gate_rows[:], 0.0)
+        for q in range(4):
+            nc.scalar.dma_start(
+                x_bytes[32 * q : 32 * q + 4, :].bitcast(I32), x_scales[0, 4 * q : 4 * q + 4, :].bitcast(I32)
+            )
+        warm = sb([P, 1], F32, "warm")
+        nc.scalar.activation(warm[:], gate_rows[:, 0:1], ACT.Sigmoid)
+
+        x_tab = sb([P, T], I32, "x_tab")
+        nc.sync.dma_start(x_tab[:], x_words[0].rearrange("p n t -> p (n t)").bitcast(I32))
+        offs_t = load_list(offs, "offs_t")
+        two_t = load_list(two, "two_t")
+        n1_t = load_list(n1, "n1_t")
+        halves = (slice(0, 256), slice(256, 512))
+        wa_raw = [sb([P, PACK, 256], F32, f"wa_raw{h}") for h in range(2)]
+        wb_raw = [sb([P, PACK, 256], F32, f"wb_raw{h}", tag=f"wb_raw{h}") for h in range(2)]
+        for h in range(2):
+            nc.sync.dma_start(wa_raw[h][:], wa.rearrange("(p j) c -> p j c", j=PACK)[:, :, halves[h]])
+        n2_t = load_list(n2, "n2_t")
+        for h in range(2):
+            nc.sync.dma_start(wb_raw[h][:], wb.rearrange("(p j) c -> p j c", j=PACK)[:, :, halves[h]])
+        for i, g in enumerate((gt, gi)):
+            nc.sync.dma_start(
+                gate_rows[4 * i : 4 * i + 4, :].rearrange("t (b r) -> t b r", r=8),
+                g.rearrange("(b t r) o -> t b (r o)", t=PACK, r=8),
+            )
+        n3_t = load_list(n3, "n3_t")
+        n4_t = load_list(n4, "n4_t")
+
+        ident = sb([P, P], F32, "ident")
+        make_identity(nc, ident[:])
+
+
+        def pick_words(words, lst):
+            nc.vector.tensor_copy(
+                words[:].rearrange("p (t b r) -> p b t r", t=PACK, r=8), x_tab[:].bitcast(U32).indirect(lst[:])
+            )
+
+        def pick_bytes(name, lst, tag=""):
+            picked = sb([P, S], U8, name + "_picked", tag=tag)
+            dealt = sb([P, S], U8, name)
+            nc.vector.tensor_copy(picked[:], x_bytes[:].indirect(lst[:]))
+            nc.vector.tensor_copy(
+                dealt[:].bitcast(I32).rearrange("p (t b r) -> p b t r", t=PACK, r=2),
+                picked[:].bitcast(I32).rearrange("p (b t r) -> p b t r", t=PACK, r=2),
+            )
+            return dealt
+
+        def quantise(grouped, codes, scales, cols):
+            nc.vector.quantize_mx(
+                out=codes[:, cols].bitcast(FP8X4),
+                scales=scales[:, cols],
+                in_=grouped[:, cols, :].rearrange("p c j -> p (c j)"),
+            )
+
+        def interleave(grouped, raw):
+            nc.scalar.copy(
+                grouped.rearrange("p (c i) j -> p c j i", i=4), raw.rearrange("p j (c i) -> p c j i", i=4)
+            )
+
+        def mx_tiles(name):
+            return sb([P, 512, PACK], BF16, name + "_g", tag=name + "_g"), sb([P, 512], U32, name + "_c"), sb([P, 512], U8, name + "_s")
+
+        def product(name, lhs_codes, lhs_scales, rhs_codes, rhs_scales, t, moving=slice(0, 512)):
+            acc = bank(name)[:, 0 : moving.stop - moving.start]
+            cols = slice(P * t, P * (t + 1))
+            nc.tensor.matmul_mx(
+                out=acc,
+                lhsT=lhs_codes[:, cols].bitcast(FP8X4),
+                lhsT_scale=lhs_scales[:, cols],
+                rhs=rhs_codes[:, moving].bitcast(FP8X4),
+                rhs_scale=rhs_scales[:, moving],
+                start=True,
+                stop=True,
+            )
+            return acc
+
+        words_a = sb([P, S], U32, "words_a")
+        pick_words(words_a, offs_t)
+        words_b = sb([P, S], U32, "words_b")
+        pick_words(words_b, two_t)
+        bytes_a = pick_bytes("bytes_a", offs_t)
+        wa_g, wa_c, wa_s = mx_tiles("wa")
+        for h in range(2):
+            interleave(wa_g[:, halves[h], :], wa_raw[h][:])
+            quantise(wa_g, wa_c, wa_s, halves[h])
+        a_sb = [sb([P, H], F32, f"a{t}") for t in range(PACK)]
+        for h in range(2):
+            acc = product(f"a_ps0{h}", words_a, bytes_a, wa_c, wa_s, 0, halves[h])
+            nc.scalar.copy(a_sb[0][:, halves[h]], acc)
+        for t in range(1, PACK):
+            acc = product(f"a_ps{t}", words_a, bytes_a, wa_c, wa_s, t)
+            nc.scalar.copy(a_sb[t][:], acc)
+        bytes_b = pick_bytes("bytes_b", two_t, tag="wa_g")
+
+        gate_ps = bank("gate_ps")
+        nc.tensor.transpose(gate_ps[:, 0:P], gate_rows[:], ident[:])
+        gates = sb([P, 8], F32, "gates")
+        nc.scalar.copy(gates[:], gate_ps[:, 0:8])
+
+        wb_g, wb_c, wb_s = mx_tiles("wb")
+        for h in range(2):
+            interleave(wb_g[:, halves[h], :], wb_raw[h][:])
+        cv_win = [sb([P, 2 * N], F32, f"cv{t}") for t in range(PACK)]
+        pairs = sb([P, PACK, 2, W], F32, "pairs")
+        for u in range(2):
+            diff = sb([P, 2, W], F32, f"diff{u}", tag=f"wb_raw{u}")
+            for t in (2 * u, 2 * u + 1):
+                nc.vector.tensor_copy(pairs[:, t, 0, :], a_sb[t][:].indirect(n1_t[:]))
+                nc.vector.tensor_copy(pairs[:, t, 1, :], a_sb[t][:].indirect(n2_t[:]))
+            both = slice(2 * u, 2 * u + 2)
+            nc.vector.tensor_tensor(diff[:], pairs[:, both, 0, :], pairs[:, both, 1, :], ALU.subtract)
+            for t in (2 * u, 2 * u + 1):
+                nc.scalar.activation(cv_win[t][:, N : N + W], diff[:, t % 2, :], ACT.Sigmoid)
+                nc.scalar.activation(cv_win[t][:, N + W :], diff[:, t % 2, :], ACT.Sigmoid, scale=-1.0)
+
+        quantise(wb_g, wb_c, wb_s, slice(0, N))
+        z2_rows = sb([P, PACK, N], BF16, "z2_rows", tag="z_g")
+        z2_g, z2_c, z2_s = mx_tiles("z2")
+        for t in range(PACK):
+            acc = product(f"b_ps{t}", words_b, bytes_b, wb_c, wb_s, t)
+            nc.scalar.activation(z2_rows[:, t, :], acc, ACT.Copy, scale=gates[:, 4 + t : 5 + t])
+        for h in range(2):
+            interleave(z2_g[:, halves[h], :], z2_rows[:, :, halves[h]])
+
+        dt = [sb([P, H], F32, f"dt{t}", tag="") for t in range(PACK)]
+        z_g, z_c, z_s = mx_tiles("z")
+
+        def scatter(t, side):
+            lst = (n1_t, n2_t)[side]
+            nc.vector.tensor_tensor(
+                dt[t][:].indirect(lst[:]), pairs[:, t, side, :], cv_win[t][:, N + side * W : N + (side + 1) * W], ALU.mult
+            )
+
+        def z_plane(t, us):
+            nc.scalar.activation(
+                z_g[:, :, t].rearrange("p (u m) -> p u m", u=PACK)[:, us, :],
+                dt[t][:].rearrange("p (m u) -> p u m", u=PACK)[:, us, :],
+                ACT.Copy,
+                scale=gates[:, t : t + 1],
+            )
+
+        scatter(0, 0)
+        for t in range(PACK - 1):
+            scatter(t + 1, 0)
+            scatter(t, 1)
+            z_plane(t, slice(0, PACK))
+        scatter(PACK - 1, 1)
+        quantise(z2_g, z2_c, z2_s, slice(0, N))
+        for u in range(PACK):
+            z_plane(PACK - 1, slice(u, u + 1))
+            quantise(z_g, z_c, z_s, slice(P * u, P * (u + 1)))
+        for h in range(2):
+            acc = product(f"cv_ps0{h}", z_c, z_s, z2_c, z2_s, 0, halves[h])
+            nc.vector.tensor_scalar(cv_win[0][:, halves[h]], acc, 0.0625, None, ALU.mult)
+        for u in range(1, PACK):
+            acc = product(f"cv_ps{u}", z_c, z_s, z2_c, z2_s, u)
+            nc.scalar.activation(cv_win[u][:, 0:N], acc, ACT.Copy, scale=0.0625)
+
+        st_win = [sb([P, 2 * N if t < PACK - 1 else N], F32, f"st{t}") for t in range(PACK)]
+        hop = sb([P, PACK, N], F32, "hop")
+        res = sb([P, PACK, N], F32, "res")
+        o_g, o_c, o_s = mx_tiles("o")
+        out_rows = out_0.rearrange("(p t) n -> p t n", t=PACK)
+        out_words = out_1[0].rearrange("p n t -> p (n t)").bitcast(I32)
+
+        def larger(t):
+            fetched = st_win[t][:, N:] if t < PACK - 1 else sb([P, N], F32, "fetched_last")[:]
+            nc.vector.tensor_copy(fetched, cv_win[t][:].indirect(n3_t[:]))
+            nc.vector.tensor_tensor(st_win[t][:, 0:N], fetched, cv_win[t][:, 0:N], ALU.max)
+
+        def smaller(t, cols):
+            nc.vector.tensor_copy(hop[:, t, cols], st_win[t][:].indirect(n4_t[:, cols.start // 16 : cols.stop // 16]))
+            nc.vector.tensor_tensor(res[:, t, cols], hop[:, t, cols], st_win[t][:, cols], ALU.min)
+            nc.scalar.copy(o_g[:, cols, t], res[:, t, cols])
+            nc.sync.dma_start(out_rows[:, t, cols], res[:, t, cols])
+
+        larger(0)
+        for t in range(PACK - 1):
+            larger(t + 1)
+            smaller(t, slice(0, N))
+        for cols in (slice(0, 256), slice(256, 384), slice(384, 512)):
+            smaller(PACK - 1, cols)
+            quantise(o_g, o_c, o_s, cols)
+            nc.sync.dma_start(out_words[:, cols], o_c[:, cols].bitcast(I32))
+        for q in range(4):
+            (nc.scalar, nc.sync)[q // 3].dma_start(
+                out_2[0, 4 * q : 4 * q + 4, :].bitcast(I32), o_s[32 * q : 32 * q + 4, :].bitcast(I32)
+            )

@@ -119,7 +119,7 @@ def tile_picked_momduelhopmn_none_po_kernel(
             )
             return acc
 
-        words_a = sb([P, S], U32, "words_a")
+        words_a = sb([P, S], U32, "words_a", tag="wb_g")
         pick_words(words_a, offs_t)
         words_b = sb([P, S], U32, "words_b")
         pick_words(words_b, two_t)
@@ -216,15 +216,20 @@ def tile_picked_momduelhopmn_none_po_kernel(
         def smaller(t, cols):
             nc.vector.tensor_copy(hop[:, t, cols], st_win[t][:].indirect(n4_t[:, cols.start // 16 : cols.stop // 16]))
             nc.vector.tensor_tensor(res[:, t, cols], hop[:, t, cols], st_win[t][:, cols], ALU.min)
-            nc.scalar.copy(o_g[:, cols, t], res[:, t, cols])
             nc.sync.dma_start(out_rows[:, t, cols], res[:, t, cols])
+
+        def round_pair(u, cols):
+            nc.scalar.copy(o_g[:, cols, 2 * u : 2 * u + 2], res[:, 2 * u : 2 * u + 2, cols].rearrange("p t n -> p n t"))
 
         larger(0)
         for t in range(PACK - 1):
             larger(t + 1)
             smaller(t, slice(0, N))
+            if t == 1:
+                round_pair(0, slice(0, N))
         for cols in (slice(0, 256), slice(256, 384), slice(384, 512)):
             smaller(PACK - 1, cols)
+            round_pair(1, cols)
             quantise(o_g, o_c, o_s, cols)
             nc.sync.dma_start(out_words[:, cols], o_c[:, cols].bitcast(I32))
         for q in range(4):

@@ -50,16 +50,16 @@ def tile_picked_momduelhopmn_none_po_kernel(
         warm = sb([P, 1], F32, "warm")
         nc.scalar.activation(warm[:], gate_rows[:, 0:1], ACT.Sigmoid)
 
-        x_tab = sb([P, T], I32, "x_tab")
-        nc.sync.dma_start(x_tab[:], x_words[0].rearrange("p n t -> p (n t)").bitcast(I32))
         offs_t = load_list(offs, "offs_t")
-        two_t = load_list(two, "two_t")
-        n1_t = load_list(n1, "n1_t")
         halves = (slice(0, 256), slice(256, 512))
         wa_raw = [sb([P, PACK, 256], F32, f"wa_raw{h}") for h in range(2)]
         wb_raw = [sb([P, PACK, 256], F32, f"wb_raw{h}", tag=f"wb_raw{h}") for h in range(2)]
         for h in range(2):
             nc.sync.dma_start(wa_raw[h][:], wa.rearrange("(p j) c -> p j c", j=PACK)[:, :, halves[h]])
+        x_tab = sb([P, T], I32, "x_tab")
+        nc.sync.dma_start(x_tab[:], x_words[0].rearrange("p n t -> p (n t)").bitcast(I32))
+        two_t = load_list(two, "two_t")
+        n1_t = load_list(n1, "n1_t")
         n2_t = load_list(n2, "n2_t")
         for h in range(2):
             nc.sync.dma_start(wb_raw[h][:], wb.rearrange("(p j) c -> p j c", j=PACK)[:, :, halves[h]])
@@ -119,15 +119,13 @@ def tile_picked_momduelhopmn_none_po_kernel(
             )
             return acc
 
-        words_a = sb([P, S], U32, "words_a", tag="wb_g")
-        pick_words(words_a, offs_t)
-        words_b = sb([P, S], U32, "words_b")
-        pick_words(words_b, two_t)
         bytes_a = pick_bytes("bytes_a", offs_t)
         wa_g, wa_c, wa_s = mx_tiles("wa")
         for h in range(2):
             interleave(wa_g[:, halves[h], :], wa_raw[h][:])
             quantise(wa_g, wa_c, wa_s, halves[h])
+        words_a = sb([P, S], U32, "words_a", tag="wb_g")
+        pick_words(words_a, offs_t)
         a_sb = [sb([P, H], F32, f"a{t}") for t in range(PACK)]
         for h in range(2):
             acc = product(f"a_ps0{h}", words_a, bytes_a, wa_c, wa_s, 0, halves[h])
@@ -135,7 +133,9 @@ def tile_picked_momduelhopmn_none_po_kernel(
         for t in range(1, PACK):
             acc = product(f"a_ps{t}", words_a, bytes_a, wa_c, wa_s, t)
             nc.scalar.copy(a_sb[t][:], acc)
-        bytes_b = pick_bytes("bytes_b", two_t, tag="wa_g")
+        bytes_b = pick_bytes("bytes_b", two_t)
+        words_b = sb([P, S], U32, "words_b")
+        pick_words(words_b, two_t)
 
         gate_ps = bank("gate_ps")
         nc.tensor.transpose(gate_ps[:, 0:P], gate_rows[:], ident[:])
@@ -216,7 +216,6 @@ def tile_picked_momduelhopmn_none_po_kernel(
         def smaller(t, cols):
             nc.vector.tensor_copy(hop[:, t, cols], st_win[t][:].indirect(n4_t[:, cols.start // 16 : cols.stop // 16]))
             nc.vector.tensor_tensor(res[:, t, cols], hop[:, t, cols], st_win[t][:, cols], ALU.min)
-            nc.sync.dma_start(out_rows[:, t, cols], res[:, t, cols])
 
         def round_pair(u, cols):
             nc.scalar.copy(o_g[:, cols, 2 * u : 2 * u + 2], res[:, 2 * u : 2 * u + 2, cols].rearrange("p t n -> p n t"))
@@ -225,13 +224,19 @@ def tile_picked_momduelhopmn_none_po_kernel(
         for t in range(PACK - 1):
             larger(t + 1)
             smaller(t, slice(0, N))
+            nc.sync.dma_start(out_rows[:, t, :], res[:, t, :])
             if t == 1:
                 round_pair(0, slice(0, N))
-        for cols in (slice(0, 256), slice(256, 384), slice(384, 512)):
+        for i, cols in enumerate((slice(0, 256), slice(256, 384), slice(384, 512))):
             smaller(PACK - 1, cols)
+            if i != 1:
+                rows = halves[i // 2]
+                nc.sync.dma_start(out_rows[:, PACK - 1, rows], res[:, PACK - 1, rows])
             round_pair(1, cols)
             quantise(o_g, o_c, o_s, cols)
-            nc.sync.dma_start(out_words[:, cols], o_c[:, cols].bitcast(I32))
+            if i != 0:
+                done = slice(0 if i == 1 else cols.start, cols.stop)
+                nc.sync.dma_start(out_words[:, done], o_c[:, done].bitcast(I32))
         for q in range(4):
             (nc.scalar, nc.sync)[q // 3].dma_start(
                 out_2[0, 4 * q : 4 * q + 4, :].bitcast(I32), o_s[32 * q : 32 * q + 4, :].bitcast(I32)

@@ -18,6 +18,17 @@ ACT = mybir.ActivationFunctionType
 
 P = 128
 PACK = 4
+LAST = PACK - 1
+RUN = 8
+QUADRANT = 32
+COLS = 512
+PSUM_BANKS = 8
+CV_SCALE = 0.0625
+ALL = slice(0, COLS)
+HALVES = (slice(0, 256), slice(256, 512))
+WA_LAST_QUARTERS = (slice(256, 384), slice(384, 512))
+TAIL_PIECES = (slice(0, 256), slice(256, 384), slice(384, 512))
+GPSIMD_MINIMA = 2
 
 
 def tile_picked_momduelhopmn_none_po_kernel(
@@ -26,47 +37,52 @@ def tile_picked_momduelhopmn_none_po_kernel(
     nc = tc.nc
     with ExitStack() as ctx:
         keep = ctx.enter_context(tc.tile_pool(name="keep", bufs=1))
-        psum = ctx.enter_context(tc.psum_pool(name="psum", bufs=8))
+        psum = ctx.enter_context(tc.psum_pool(name="psum", bufs=PSUM_BANKS))
 
         def sb(shape, dtype, name, tag=""):
             return keep.tile(shape, dtype, name=name, tag=tag, align_bytes=64)
 
         def bank(name):
-            return psum.tile([P, 512], F32, name=name, tag="bank")
+            return psum.tile([P, COLS], F32, name=name, tag="bank")
 
         def load_list(src, name):
             tile = keep.tile(list(src.shape), U16, name=name)
             nc.sync.dma_start(tile[:], src)
             return tile
 
+        def scale_rows(tile, quadrant):
+            return tile[QUADRANT * quadrant : QUADRANT * quadrant + 4, :].bitcast(I32)
+
+        def k_rows(w, cols):
+            return w.rearrange("(p j) c -> p j c", j=PACK)[:, :, cols]
+
         x_bytes = sb([P, T], U8, "x_bytes")
         nc.vector.memset(x_bytes[:].bitcast(I32), 0)
         gate_rows = sb([P, P], F32, "gate_rows")
         nc.vector.memset(gate_rows[:], 0.0)
-        for q in range(4):
-            nc.scalar.dma_start(
-                x_bytes[32 * q : 32 * q + 4, :].bitcast(I32), x_scales[0, 4 * q : 4 * q + 4, :].bitcast(I32)
+        for quadrant in range(4):
+            nc.sync.dma_start(
+                scale_rows(x_bytes, quadrant), x_scales[0, 4 * quadrant : 4 * quadrant + 4, :].bitcast(I32)
             )
         warm = sb([P, 1], F32, "warm")
         nc.scalar.activation(warm[:], gate_rows[:, 0:1], ACT.Sigmoid)
 
         offs_t = load_list(offs, "offs_t")
-        halves = (slice(0, 256), slice(256, 512))
-        wa_raw = [sb([P, PACK, 256], F32, f"wa_raw{h}") for h in range(2)]
-        wb_raw = [sb([P, PACK, 256], F32, f"wb_raw{h}", tag=f"wb_raw{h}") for h in range(2)]
-        for h in range(2):
-            nc.sync.dma_start(wa_raw[h][:], wa.rearrange("(p j) c -> p j c", j=PACK)[:, :, halves[h]])
-        x_tab = sb([P, T], I32, "x_tab")
-        nc.sync.dma_start(x_tab[:], x_words[0].rearrange("p n t -> p (n t)").bitcast(I32))
         two_t = load_list(two, "two_t")
         n1_t = load_list(n1, "n1_t")
+        wa_raw = [sb([P, PACK, 256], F32, f"wa_raw{h}", tag=f"wa_raw{h}") for h in range(2)]
+        wb_raw = [sb([P, PACK, 256], F32, f"wb_raw{h}", tag=f"wb_raw{h}") for h in range(2)]
+        x_tab = sb([P, T], I32, "x_tab")
+        nc.sync.dma_start(wa_raw[0][:], k_rows(wa, HALVES[0]))
+        nc.sync.dma_start(x_tab[:], x_words[0].rearrange("p n t -> p (n t)").bitcast(I32))
+        nc.sync.dma_start(wa_raw[1][:], k_rows(wa, HALVES[1]))
         n2_t = load_list(n2, "n2_t")
         for h in range(2):
-            nc.sync.dma_start(wb_raw[h][:], wb.rearrange("(p j) c -> p j c", j=PACK)[:, :, halves[h]])
-        for i, g in enumerate((gt, gi)):
+            nc.sync.dma_start(wb_raw[h][:], k_rows(wb, HALVES[h]))
+        for i, gate in enumerate((gt, gi)):
             nc.sync.dma_start(
-                gate_rows[4 * i : 4 * i + 4, :].rearrange("t (b r) -> t b r", r=8),
-                g.rearrange("(b t r) o -> t b (r o)", t=PACK, r=8),
+                gate_rows[PACK * i : PACK * (i + 1), :].rearrange("t (b r) -> t b r", r=RUN),
+                gate.rearrange("(b t r) o -> t b (r o)", t=PACK, r=RUN),
             )
         n3_t = load_list(n3, "n3_t")
         n4_t = load_list(n4, "n4_t")
@@ -74,21 +90,27 @@ def tile_picked_momduelhopmn_none_po_kernel(
         ident = sb([P, P], F32, "ident")
         make_identity(nc, ident[:])
 
-
         def pick_words(words, lst):
             nc.vector.tensor_copy(
-                words[:].rearrange("p (t b r) -> p b t r", t=PACK, r=8), x_tab[:].bitcast(U32).indirect(lst[:])
+                words[:].rearrange("p (t b r) -> p b t r", t=PACK, r=RUN), x_tab[:].bitcast(U32).indirect(lst[:])
             )
 
-        def pick_bytes(name, lst, tag=""):
-            picked = sb([P, S], U8, name + "_picked", tag=tag)
+        def pick_bytes(name, lst):
+            picked = sb([P, S], U8, name + "_picked")
             dealt = sb([P, S], U8, name)
             nc.vector.tensor_copy(picked[:], x_bytes[:].indirect(lst[:]))
             nc.vector.tensor_copy(
-                dealt[:].bitcast(I32).rearrange("p (t b r) -> p b t r", t=PACK, r=2),
-                picked[:].bitcast(I32).rearrange("p (b t r) -> p b t r", t=PACK, r=2),
+                dealt[:].bitcast(I32).rearrange("p (t b r) -> p b t r", t=PACK, r=RUN // 4),
+                picked[:].bitcast(I32).rearrange("p (b t r) -> p b t r", t=PACK, r=RUN // 4),
             )
             return dealt
+
+        def mx_tiles(name):
+            grouped = sb([P, COLS, PACK], BF16, name + "_g", tag=name + "_g")
+            return grouped, sb([P, COLS], U32, name + "_c"), sb([P, COLS], U8, name + "_s")
+
+        def interleave(copy, grouped, rows):
+            copy(grouped.rearrange("p (c i) j -> p c j i", i=4), rows.rearrange("p j (c i) -> p c j i", i=4))
 
         def quantise(grouped, codes, scales, cols):
             nc.vector.quantize_mx(
@@ -97,21 +119,13 @@ def tile_picked_momduelhopmn_none_po_kernel(
                 in_=grouped[:, cols, :].rearrange("p c j -> p (c j)"),
             )
 
-        def interleave(grouped, raw):
-            nc.scalar.copy(
-                grouped.rearrange("p (c i) j -> p c j i", i=4), raw.rearrange("p j (c i) -> p c j i", i=4)
-            )
-
-        def mx_tiles(name):
-            return sb([P, 512, PACK], BF16, name + "_g", tag=name + "_g"), sb([P, 512], U32, name + "_c"), sb([P, 512], U8, name + "_s")
-
-        def product(name, lhs_codes, lhs_scales, rhs_codes, rhs_scales, t, moving=slice(0, 512)):
+        def product(name, lhs_codes, lhs_scales, rhs_codes, rhs_scales, t, moving=ALL):
             acc = bank(name)[:, 0 : moving.stop - moving.start]
-            cols = slice(P * t, P * (t + 1))
+            stationary = slice(P * t, P * (t + 1))
             nc.tensor.matmul_mx(
                 out=acc,
-                lhsT=lhs_codes[:, cols].bitcast(FP8X4),
-                lhsT_scale=lhs_scales[:, cols],
+                lhsT=lhs_codes[:, stationary].bitcast(FP8X4),
+                lhsT_scale=lhs_scales[:, stationary],
                 rhs=rhs_codes[:, moving].bitcast(FP8X4),
                 rhs_scale=rhs_scales[:, moving],
                 start=True,
@@ -121,30 +135,33 @@ def tile_picked_momduelhopmn_none_po_kernel(
 
         bytes_a = pick_bytes("bytes_a", offs_t)
         wa_g, wa_c, wa_s = mx_tiles("wa")
-        for h in range(2):
-            interleave(wa_g[:, halves[h], :], wa_raw[h][:])
-            quantise(wa_g, wa_c, wa_s, halves[h])
+        interleave(nc.scalar.copy, wa_g[:, HALVES[0], :], wa_raw[0][:])
+        quantise(wa_g, wa_c, wa_s, HALVES[0])
+        for copy, cols in zip((nc.scalar.copy, nc.vector.tensor_copy), WA_LAST_QUARTERS):
+            interleave(copy, wa_g[:, cols, :], wa_raw[1][:, :, cols.start - 256 : cols.stop - 256])
+        quantise(wa_g, wa_c, wa_s, HALVES[1])
         words_a = sb([P, S], U32, "words_a", tag="wb_g")
         pick_words(words_a, offs_t)
-        a_sb = [sb([P, H], F32, f"a{t}") for t in range(PACK)]
+        a_sb = [sb([P, H], F32, f"a{t}", tag="wa_raw1" if t == 0 else "") for t in range(PACK)]
         for h in range(2):
-            acc = product(f"a_ps0{h}", words_a, bytes_a, wa_c, wa_s, 0, halves[h])
-            nc.scalar.copy(a_sb[0][:, halves[h]], acc)
+            acc = product(f"a_ps0{h}", words_a, bytes_a, wa_c, wa_s, 0, HALVES[h])
+            nc.scalar.copy(a_sb[0][:, HALVES[h]], acc)
         for t in range(1, PACK):
             acc = product(f"a_ps{t}", words_a, bytes_a, wa_c, wa_s, t)
             nc.scalar.copy(a_sb[t][:], acc)
         bytes_b = pick_bytes("bytes_b", two_t)
-        words_b = sb([P, S], U32, "words_b")
+        words_b = sb([P, S], U32, "words_b", tag="wa_g")
         pick_words(words_b, two_t)
 
         gate_ps = bank("gate_ps")
         nc.tensor.transpose(gate_ps[:, 0:P], gate_rows[:], ident[:])
-        gates = sb([P, 8], F32, "gates")
-        nc.scalar.copy(gates[:], gate_ps[:, 0:8])
+        gates = sb([P, 2 * PACK], F32, "gates")
+        nc.scalar.copy(gates[:], gate_ps[:, 0 : 2 * PACK])
 
         wb_g, wb_c, wb_s = mx_tiles("wb")
         for h in range(2):
-            interleave(wb_g[:, halves[h], :], wb_raw[h][:])
+            interleave(nc.scalar.copy, wb_g[:, HALVES[h], :], wb_raw[h][:])
+
         cv_win = [sb([P, 2 * N], F32, f"cv{t}") for t in range(PACK)]
         pairs = sb([P, PACK, 2, W], F32, "pairs")
         for u in range(2):
@@ -152,31 +169,30 @@ def tile_picked_momduelhopmn_none_po_kernel(
             for t in (2 * u, 2 * u + 1):
                 nc.vector.tensor_copy(pairs[:, t, 0, :], a_sb[t][:].indirect(n1_t[:]))
                 nc.vector.tensor_copy(pairs[:, t, 1, :], a_sb[t][:].indirect(n2_t[:]))
-            both = slice(2 * u, 2 * u + 2)
-            nc.vector.tensor_tensor(diff[:], pairs[:, both, 0, :], pairs[:, both, 1, :], ALU.subtract)
             for t in (2 * u, 2 * u + 1):
+                engine = nc.vector if t == LAST else nc.gpsimd
+                engine.tensor_tensor(diff[:, t % 2, :], pairs[:, t, 0, :], pairs[:, t, 1, :], ALU.subtract)
                 nc.scalar.activation(cv_win[t][:, N : N + W], diff[:, t % 2, :], ACT.Sigmoid)
                 nc.scalar.activation(cv_win[t][:, N + W :], diff[:, t % 2, :], ACT.Sigmoid, scale=-1.0)
 
-        quantise(wb_g, wb_c, wb_s, slice(0, N))
+        quantise(wb_g, wb_c, wb_s, ALL)
         z2_rows = sb([P, PACK, N], BF16, "z2_rows", tag="z_g")
         z2_g, z2_c, z2_s = mx_tiles("z2")
         for t in range(PACK):
             acc = product(f"b_ps{t}", words_b, bytes_b, wb_c, wb_s, t)
-            nc.scalar.activation(z2_rows[:, t, :], acc, ACT.Copy, scale=gates[:, 4 + t : 5 + t])
+            nc.scalar.activation(z2_rows[:, t, :], acc, ACT.Copy, scale=gates[:, PACK + t : PACK + t + 1])
         for h in range(2):
-            interleave(z2_g[:, halves[h], :], z2_rows[:, :, halves[h]])
+            interleave(nc.scalar.copy, z2_g[:, HALVES[h], :], z2_rows[:, :, HALVES[h]])
 
-        dt = [sb([P, H], F32, f"dt{t}", tag="") for t in range(PACK)]
+        dt = [sb([P, H], F32, f"dt{t}") for t in range(PACK)]
         z_g, z_c, z_s = mx_tiles("z")
 
         def scatter(t, side):
             lst = (n1_t, n2_t)[side]
-            nc.vector.tensor_tensor(
-                dt[t][:].indirect(lst[:]), pairs[:, t, side, :], cv_win[t][:, N + side * W : N + (side + 1) * W], ALU.mult
-            )
+            weight = cv_win[t][:, N + side * W : N + (side + 1) * W]
+            nc.vector.tensor_tensor(dt[t][:].indirect(lst[:]), pairs[:, t, side, :], weight, ALU.mult)
 
-        def z_plane(t, us):
+        def round_z(t, us):
             nc.scalar.activation(
                 z_g[:, :, t].rearrange("p (u m) -> p u m", u=PACK)[:, us, :],
                 dt[t][:].rearrange("p (m u) -> p u m", u=PACK)[:, us, :],
@@ -185,23 +201,25 @@ def tile_picked_momduelhopmn_none_po_kernel(
             )
 
         scatter(0, 0)
-        for t in range(PACK - 1):
+        for t in range(LAST):
             scatter(t + 1, 0)
             scatter(t, 1)
-            z_plane(t, slice(0, PACK))
-        scatter(PACK - 1, 1)
-        quantise(z2_g, z2_c, z2_s, slice(0, N))
+            round_z(t, slice(0, PACK))
+        scatter(LAST, 1)
+        quantise(z2_g, z2_c, z2_s, ALL)
         for u in range(PACK):
-            z_plane(PACK - 1, slice(u, u + 1))
+            round_z(LAST, slice(u, u + 1))
             quantise(z_g, z_c, z_s, slice(P * u, P * (u + 1)))
-        for h in range(2):
-            acc = product(f"cv_ps0{h}", z_c, z_s, z2_c, z2_s, 0, halves[h])
-            nc.vector.tensor_scalar(cv_win[0][:, halves[h]], acc, 0.0625, None, ALU.mult)
-        for u in range(1, PACK):
-            acc = product(f"cv_ps{u}", z_c, z_s, z2_c, z2_s, u)
-            nc.scalar.activation(cv_win[u][:, 0:N], acc, ACT.Copy, scale=0.0625)
 
-        st_win = [sb([P, 2 * N if t < PACK - 1 else N], F32, f"st{t}") for t in range(PACK)]
+        for h in range(2):
+            acc = product(f"cv_ps0{h}", z_c, z_s, z2_c, z2_s, 0, HALVES[h])
+            nc.vector.tensor_scalar(cv_win[0][:, HALVES[h]], acc, CV_SCALE, None, ALU.mult)
+        cv_ps = {}
+        for t in range(1, PACK):
+            cv_ps[t] = product(f"cv_ps{t}", z_c, z_s, z2_c, z2_s, t)
+            nc.scalar.activation(cv_win[t][:, 0:N], cv_ps[t], ACT.Copy, scale=CV_SCALE)
+
+        st_win = [sb([P, 2 * N if t < LAST else N], F32, f"st{t}") for t in range(PACK)]
         hop = sb([P, PACK, N], F32, "hop")
         res = sb([P, PACK, N], F32, "res")
         o_g, o_c, o_s = mx_tiles("o")
@@ -209,35 +227,48 @@ def tile_picked_momduelhopmn_none_po_kernel(
         out_words = out_1[0].rearrange("p n t -> p (n t)").bitcast(I32)
 
         def larger(t):
-            fetched = st_win[t][:, N:] if t < PACK - 1 else sb([P, N], F32, "fetched_last")[:]
+            fetched = st_win[t][:, N:] if t < LAST else sb([P, N], F32, "fetched_last")[:]
             nc.vector.tensor_copy(fetched, cv_win[t][:].indirect(n3_t[:]))
-            nc.vector.tensor_tensor(st_win[t][:, 0:N], fetched, cv_win[t][:, 0:N], ALU.max)
+            if t == 0:
+                nc.vector.tensor_tensor(st_win[t][:, 0:N], fetched, cv_win[t][:, 0:N], ALU.max)
+            else:
+                nc.vector.scalar_tensor_tensor(st_win[t][:, 0:N], cv_ps[t], CV_SCALE, fetched, ALU.mult, ALU.max)
 
         def smaller(t, cols):
             nc.vector.tensor_copy(hop[:, t, cols], st_win[t][:].indirect(n4_t[:, cols.start // 16 : cols.stop // 16]))
-            nc.vector.tensor_tensor(res[:, t, cols], hop[:, t, cols], st_win[t][:, cols], ALU.min)
+            if t < GPSIMD_MINIMA:
+                excess = sb([P, N], F32, f"excess{t}")
+                nc.gpsimd.tensor_tensor(excess[:], st_win[t][:, cols], hop[:, t, cols], ALU.subtract)
+                nc.scalar.activation(hop[:, t, cols], excess[:], ACT.Relu)
+                nc.gpsimd.tensor_tensor(res[:, t, cols], st_win[t][:, cols], hop[:, t, cols], ALU.subtract)
+            else:
+                nc.vector.tensor_tensor(res[:, t, cols], hop[:, t, cols], st_win[t][:, cols], ALU.min)
 
-        def round_pair(u, cols):
-            nc.scalar.copy(o_g[:, cols, 2 * u : 2 * u + 2], res[:, 2 * u : 2 * u + 2, cols].rearrange("p t n -> p n t"))
+        def round_out(copy, u, cols):
+            copy(o_g[:, cols, 2 * u : 2 * u + 2], res[:, 2 * u : 2 * u + 2, cols].rearrange("p t n -> p n t"))
 
         larger(0)
-        for t in range(PACK - 1):
+        for t in range(LAST):
             larger(t + 1)
-            smaller(t, slice(0, N))
+            smaller(t, ALL)
             nc.sync.dma_start(out_rows[:, t, :], res[:, t, :])
             if t == 1:
-                round_pair(0, slice(0, N))
-        for i, cols in enumerate((slice(0, 256), slice(256, 384), slice(384, 512))):
-            smaller(PACK - 1, cols)
-            if i != 1:
-                rows = halves[i // 2]
-                nc.sync.dma_start(out_rows[:, PACK - 1, rows], res[:, PACK - 1, rows])
-            round_pair(1, cols)
-            quantise(o_g, o_c, o_s, cols)
-            if i != 0:
-                done = slice(0 if i == 1 else cols.start, cols.stop)
-                nc.sync.dma_start(out_words[:, done], o_c[:, done].bitcast(I32))
-        for q in range(4):
-            (nc.scalar, nc.sync)[q // 3].dma_start(
-                out_2[0, 4 * q : 4 * q + 4, :].bitcast(I32), o_s[32 * q : 32 * q + 4, :].bitcast(I32)
+                round_out(nc.scalar.copy, 0, ALL)
+        first, middle, final = TAIL_PIECES
+        smaller(LAST, first)
+        nc.sync.dma_start(out_rows[:, LAST, HALVES[0]], res[:, LAST, HALVES[0]])
+        round_out(nc.scalar.copy, 1, first)
+        quantise(o_g, o_c, o_s, first)
+        smaller(LAST, middle)
+        round_out(nc.scalar.copy, 1, middle)
+        quantise(o_g, o_c, o_s, middle)
+        nc.sync.dma_start(out_words[:, 0 : middle.stop], o_c[:, 0 : middle.stop].bitcast(I32))
+        smaller(LAST, final)
+        nc.sync.dma_start(out_rows[:, LAST, HALVES[1]], res[:, LAST, HALVES[1]])
+        round_out(nc.vector.tensor_copy, 1, final)
+        quantise(o_g, o_c, o_s, final)
+        nc.sync.dma_start(out_words[:, final], o_c[:, final].bitcast(I32))
+        for quadrant in range(4):
+            (nc.scalar, nc.sync)[quadrant // 2].dma_start(
+                out_2[0, 4 * quadrant : 4 * quadrant + 4, :].bitcast(I32), scale_rows(o_s, quadrant)
             )

from contextlib import ExitStack

import concourse.mybir as mybir
from concourse.masks import make_identity

K, T, S, N, H, W = 512, 2048, 512, 512, 512, 256
FLOPS = 2 * K * S * H + 2 * K * S * N + 2 * S * H * N

F32 = mybir.dt.float32
BF16 = mybir.dt.bfloat16
I32 = mybir.dt.int32
U32 = mybir.dt.uint32
U16 = mybir.dt.uint16
U8 = mybir.dt.uint8
FP8X4 = mybir.dt.float8_e4m3fn_x4
ALU = mybir.AluOpType
ACT = mybir.ActivationFunctionType

P = 128
PACK = 4
LAST = PACK - 1
RUN = 8
QUADRANT = 32
COLS = 512
PSUM_BANKS = 8
CV_SCALE = 0.0625
ALL = slice(0, COLS)
HALVES = (slice(0, 256), slice(256, 512))
WA_LAST_QUARTERS = (slice(256, 384), slice(384, 512))
TAIL_PIECES = (slice(0, 256), slice(256, 384), slice(384, 512))
GPSIMD_MINIMA = 2


def tile_picked_momduelhopmn_none_po_kernel(
    tc, x_words, x_scales, wa, wb, gt, gi, offs, two, n1, n2, n3, n4, out_0, out_1, out_2
):
    nc = tc.nc
    with ExitStack() as ctx:
        keep = ctx.enter_context(tc.tile_pool(name="keep", bufs=1))
        psum = ctx.enter_context(tc.psum_pool(name="psum", bufs=PSUM_BANKS))

        def sb(shape, dtype, name, tag=""):
            return keep.tile(shape, dtype, name=name, tag=tag, align_bytes=64)

        def bank(name):
            return psum.tile([P, COLS], F32, name=name, tag="bank")

        def load_list(src, name):
            tile = keep.tile(list(src.shape), U16, name=name)
            nc.sync.dma_start(tile[:], src)
            return tile

        def scale_rows(tile, quadrant):
            return tile[QUADRANT * quadrant : QUADRANT * quadrant + 4, :].bitcast(I32)

        def k_rows(w, cols):
            return w.rearrange("(p j) c -> p j c", j=PACK)[:, :, cols]

        x_bytes = sb([P, T], U8, "x_bytes")
        nc.vector.memset(x_bytes[:].bitcast(I32), 0)
        gate_rows = sb([P, P], F32, "gate_rows")
        nc.vector.memset(gate_rows[:], 0.0)
        for quadrant in range(4):
            nc.sync.dma_start(
                scale_rows(x_bytes, quadrant), x_scales[0, 4 * quadrant : 4 * quadrant + 4, :].bitcast(I32)
            )
        warm = sb([P, 1], F32, "warm")
        nc.scalar.activation(warm[:], gate_rows[:, 0:1], ACT.Sigmoid)

        offs_t = load_list(offs, "offs_t")
        two_t = load_list(two, "two_t")
        n1_t = load_list(n1, "n1_t")
        wa_raw = [sb([P, PACK, 256], F32, f"wa_raw{h}", tag=f"wa_raw{h}") for h in range(2)]
        wb_raw = [sb([P, PACK, 256], F32, f"wb_raw{h}", tag=f"wb_raw{h}") for h in range(2)]
        x_tab = sb([P, T], I32, "x_tab")
        nc.sync.dma_start(wa_raw[0][:], k_rows(wa, HALVES[0]))
        nc.sync.dma_start(x_tab[:], x_words[0].rearrange("p n t -> p (n t)").bitcast(I32))
        nc.sync.dma_start(wa_raw[1][:], k_rows(wa, HALVES[1]))
        n2_t = load_list(n2, "n2_t")
        for h in range(2):
            nc.sync.dma_start(wb_raw[h][:], k_rows(wb, HALVES[h]))
        for i, gate in enumerate((gt, gi)):
            nc.sync.dma_start(
                gate_rows[PACK * i : PACK * (i + 1), :].rearrange("t (b r) -> t b r", r=RUN),
                gate.rearrange("(b t r) o -> t b (r o)", t=PACK, r=RUN),
            )
        n3_t = load_list(n3, "n3_t")
        n4_t = load_list(n4, "n4_t")

        ident = sb([P, P], F32, "ident")
        make_identity(nc, ident[:])

        def pick_words(words, lst):
            nc.vector.tensor_copy(
                words[:].rearrange("p (t b r) -> p b t r", t=PACK, r=RUN), x_tab[:].bitcast(U32).indirect(lst[:])
            )

        def pick_bytes(name, lst):
            picked = sb([P, S], U8, name + "_picked")
            dealt = sb([P, S], U8, name)
            nc.vector.tensor_copy(picked[:], x_bytes[:].indirect(lst[:]))
            nc.vector.tensor_copy(
                dealt[:].bitcast(I32).rearrange("p (t b r) -> p b t r", t=PACK, r=RUN // 4),
                picked[:].bitcast(I32).rearrange("p (b t r) -> p b t r", t=PACK, r=RUN // 4),
            )
            return dealt

        def mx_tiles(name):
            grouped = sb([P, COLS, PACK], BF16, name + "_g", tag=name + "_g")
            return grouped, sb([P, COLS], U32, name + "_c"), sb([P, COLS], U8, name + "_s")

        def interleave(copy, grouped, rows):
            copy(grouped.rearrange("p (c i) j -> p c j i", i=4), rows.rearrange("p j (c i) -> p c j i", i=4))

        def quantise(grouped, codes, scales, cols):
            nc.vector.quantize_mx(
                out=codes[:, cols].bitcast(FP8X4),
                scales=scales[:, cols],
                in_=grouped[:, cols, :].rearrange("p c j -> p (c j)"),
            )

        def product(name, lhs_codes, lhs_scales, rhs_codes, rhs_scales, t, moving=ALL):
            acc = bank(name)[:, 0 : moving.stop - moving.start]
            stationary = slice(P * t, P * (t + 1))
            nc.tensor.matmul_mx(
                out=acc,
                lhsT=lhs_codes[:, stationary].bitcast(FP8X4),
                lhsT_scale=lhs_scales[:, stationary],
                rhs=rhs_codes[:, moving].bitcast(FP8X4),
                rhs_scale=rhs_scales[:, moving],
                start=True,
                stop=True,
            )
            return acc

        bytes_a = pick_bytes("bytes_a", offs_t)
        wa_g, wa_c, wa_s = mx_tiles("wa")
        interleave(nc.scalar.copy, wa_g[:, HALVES[0], :], wa_raw[0][:])
        quantise(wa_g, wa_c, wa_s, HALVES[0])
        for copy, cols in zip((nc.scalar.copy, nc.vector.tensor_copy), WA_LAST_QUARTERS):
            interleave(copy, wa_g[:, cols, :], wa_raw[1][:, :, cols.start - 256 : cols.stop - 256])
        quantise(wa_g, wa_c, wa_s, HALVES[1])
        words_a = sb([P, S], U32, "words_a", tag="wb_g")
        pick_words(words_a, offs_t)
        a_sb = [sb([P, H], F32, f"a{t}", tag="wa_raw1" if t == 0 else "") for t in range(PACK)]
        for h in range(2):
            acc = product(f"a_ps0{h}", words_a, bytes_a, wa_c, wa_s, 0, HALVES[h])
            nc.scalar.copy(a_sb[0][:, HALVES[h]], acc)
        for t in range(1, PACK):
            acc = product(f"a_ps{t}", words_a, bytes_a, wa_c, wa_s, t)
            nc.scalar.copy(a_sb[t][:], acc)
        bytes_b = pick_bytes("bytes_b", two_t)
        words_b = sb([P, S], U32, "words_b", tag="wa_g")
        pick_words(words_b, two_t)

        gate_ps = bank("gate_ps")
        nc.tensor.transpose(gate_ps[:, 0:P], gate_rows[:], ident[:])
        gates = sb([P, 2 * PACK], F32, "gates")
        nc.scalar.copy(gates[:], gate_ps[:, 0 : 2 * PACK])

        wb_g, wb_c, wb_s = mx_tiles("wb")
        for h in range(2):
            interleave(nc.scalar.copy, wb_g[:, HALVES[h], :], wb_raw[h][:])

        cv_win = [sb([P, 2 * N], F32, f"cv{t}") for t in range(PACK)]
        pairs = sb([P, PACK, 2, W], F32, "pairs")
        for u in range(2):
            diff = sb([P, 2, W], F32, f"diff{u}", tag=f"wb_raw{u}")
            for t in (2 * u, 2 * u + 1):
                nc.vector.tensor_copy(pairs[:, t, 0, :], a_sb[t][:].indirect(n1_t[:]))
                nc.vector.tensor_copy(pairs[:, t, 1, :], a_sb[t][:].indirect(n2_t[:]))
            for t in (2 * u, 2 * u + 1):
                engine = nc.vector if t == LAST else nc.gpsimd
                engine.tensor_tensor(diff[:, t % 2, :], pairs[:, t, 0, :], pairs[:, t, 1, :], ALU.subtract)
                nc.scalar.activation(cv_win[t][:, N : N + W], diff[:, t % 2, :], ACT.Sigmoid)
                nc.scalar.activation(cv_win[t][:, N + W :], diff[:, t % 2, :], ACT.Sigmoid, scale=-1.0)

        quantise(wb_g, wb_c, wb_s, ALL)
        z2_rows = sb([P, PACK, N], BF16, "z2_rows", tag="z_g")
        z2_g, z2_c, z2_s = mx_tiles("z2")
        for t in range(PACK):
            acc = product(f"b_ps{t}", words_b, bytes_b, wb_c, wb_s, t)
            nc.scalar.activation(z2_rows[:, t, :], acc, ACT.Copy, scale=gates[:, PACK + t : PACK + t + 1])
        for h in range(2):
            interleave(nc.scalar.copy, z2_g[:, HALVES[h], :], z2_rows[:, :, HALVES[h]])

        dt = [sb([P, H], F32, f"dt{t}") for t in range(PACK)]
        z_g, z_c, z_s = mx_tiles("z")

        def scatter(t, side):
            lst = (n1_t, n2_t)[side]
            weight = cv_win[t][:, N + side * W : N + (side + 1) * W]
            nc.vector.tensor_tensor(dt[t][:].indirect(lst[:]), pairs[:, t, side, :], weight, ALU.mult)

        def round_z(t, us):
            nc.scalar.activation(
                z_g[:, :, t].rearrange("p (u m) -> p u m", u=PACK)[:, us, :],
                dt[t][:].rearrange("p (m u) -> p u m", u=PACK)[:, us, :],
                ACT.Copy,
                scale=gates[:, t : t + 1],
            )

        scatter(0, 0)
        for t in range(LAST):
            scatter(t + 1, 0)
            scatter(t, 1)
            round_z(t, slice(0, PACK))
        scatter(LAST, 1)
        quantise(z2_g, z2_c, z2_s, ALL)
        for u in range(PACK):
            round_z(LAST, slice(u, u + 1))
            quantise(z_g, z_c, z_s, slice(P * u, P * (u + 1)))

        for h in range(2):
            acc = product(f"cv_ps0{h}", z_c, z_s, z2_c, z2_s, 0, HALVES[h])
            nc.vector.tensor_scalar(cv_win[0][:, HALVES[h]], acc, CV_SCALE, None, ALU.mult)
        cv_ps = {}
        for t in range(1, PACK):
            cv_ps[t] = product(f"cv_ps{t}", z_c, z_s, z2_c, z2_s, t)
            nc.scalar.activation(cv_win[t][:, 0:N], cv_ps[t], ACT.Copy, scale=CV_SCALE)

        st_win = [sb([P, 2 * N if t < LAST else N], F32, f"st{t}") for t in range(PACK)]
        hop = sb([P, PACK, N], F32, "hop")
        res = sb([P, PACK, N], F32, "res")
        o_g, o_c, o_s = mx_tiles("o")
        out_rows = out_0.rearrange("(p t) n -> p t n", t=PACK)
        out_words = out_1[0].rearrange("p n t -> p (n t)").bitcast(I32)

        def larger(t):
            fetched = st_win[t][:, N:] if t < LAST else sb([P, N], F32, "fetched_last")[:]
            nc.vector.tensor_copy(fetched, cv_win[t][:].indirect(n3_t[:]))
            if t == 0:
                nc.vector.tensor_tensor(st_win[t][:, 0:N], fetched, cv_win[t][:, 0:N], ALU.max)
            else:
                nc.vector.scalar_tensor_tensor(st_win[t][:, 0:N], cv_ps[t], CV_SCALE, fetched, ALU.mult, ALU.max)

        def smaller(t, cols):
            nc.vector.tensor_copy(hop[:, t, cols], st_win[t][:].indirect(n4_t[:, cols.start // 16 : cols.stop // 16]))
            if t < GPSIMD_MINIMA:
                excess = sb([P, N], F32, f"excess{t}")
                nc.gpsimd.tensor_tensor(excess[:], st_win[t][:, cols], hop[:, t, cols], ALU.subtract)
                nc.scalar.activation(hop[:, t, cols], excess[:], ACT.Relu)
                nc.gpsimd.tensor_tensor(res[:, t, cols], st_win[t][:, cols], hop[:, t, cols], ALU.subtract)
            else:
                nc.vector.tensor_tensor(res[:, t, cols], hop[:, t, cols], st_win[t][:, cols], ALU.min)

        def round_out(copy, u, cols):
            copy(o_g[:, cols, 2 * u : 2 * u + 2], res[:, 2 * u : 2 * u + 2, cols].rearrange("p t n -> p n t"))

        larger(0)
        for t in range(LAST):
            larger(t + 1)
            smaller(t, ALL)
            nc.sync.dma_start(out_rows[:, t, :], res[:, t, :])
            if t == 1:
                round_out(nc.scalar.copy, 0, ALL)
        first, middle, final = TAIL_PIECES
        smaller(LAST, first)
        nc.sync.dma_start(out_rows[:, LAST, HALVES[0]], res[:, LAST, HALVES[0]])
        round_out(nc.scalar.copy, 1, first)
        quantise(o_g, o_c, o_s, first)
        smaller(LAST, middle)
        round_out(nc.scalar.copy, 1, middle)
        quantise(o_g, o_c, o_s, middle)
        nc.sync.dma_start(out_words[:, 0 : middle.stop], o_c[:, 0 : middle.stop].bitcast(I32))
        smaller(LAST, final)
        nc.sync.dma_start(out_rows[:, LAST, HALVES[1]], res[:, LAST, HALVES[1]])
        round_out(nc.vector.tensor_copy, 1, final)
        quantise(o_g, o_c, o_s, final)
        nc.sync.dma_start(out_words[:, final], o_c[:, final].bitcast(I32))
        for quadrant in range(4):
            (nc.scalar, nc.sync)[quadrant // 2].dma_start(
                out_2[0, 4 * quadrant : 4 * quadrant + 4, :].bitcast(I32), scale_rows(o_s, quadrant)
            )
